import numpy as np
import ml_dtypes


def mxq(x, axis, fmt="e4m3"):
    dtype, down = {"e4m3": (ml_dtypes.float8_e4m3fn, 7), "e5m2": (ml_dtypes.float8_e5m2, 14)}[fmt]
    v = np.moveaxis(np.asarray(x, np.float32).astype(ml_dtypes.bfloat16).astype(np.float64), axis, -1)
    blocks = v.reshape(v.shape[:-1] + (-1, 32))
    amax = np.abs(blocks).max(-1, keepdims=True)
    byte = np.maximum(np.where(amax > 0, np.frexp(amax)[1] - 1 + 127, 0) - down, 1)
    scale = np.exp2(byte - 127.0)
    codes = (blocks / scale).astype(np.float32).astype(dtype).astype(np.float64)
    return np.moveaxis((codes * scale).reshape(v.shape), -1, axis)


WIDE = False


def mx_kscale(k):
    if not WIDE:
        return np.ones(k)
    levels = np.array([30, -30])
    if k % 512:
        return np.exp2(np.random.permutation(np.resize(levels, k // 32))).repeat(32)
    a = np.empty((k // 512, 16))
    for p in range(k // 512):
        a[p, :8] = np.random.permutation(np.resize(levels, 8))
        for g in range(8):
            far = levels[np.abs(levels - a[p, g]) >= 10]
            a[p, g + 8] = far[np.random.randint(len(far))]
    return np.exp2(a.ravel()).repeat(32)


def f64(x):
    return np.asarray(x).astype(np.float64)


def striped(idx):
    return np.tile(np.asarray(idx).reshape(-1, 16).T, (8, 1)).astype(np.uint16)


def unstriped(offs):
    return offs[:16].T.reshape(-1).astype(np.int64)


E2M1 = np.array([0.0, 0.5, 1.0, 1.5, 2.0, 3.0, 4.0, 6.0, -0.0, -0.5, -1.0, -1.5, -2.0, -3.0, -4.0, -6.0])


def pack_weight(w, fmt):
    k, n = w.shape
    w = f64(np.asarray(w, np.float32).astype(ml_dtypes.bfloat16)).reshape(k // 32, 32, n)
    amax = np.abs(w).max(1)
    if fmt in ("e4m3", "e5m2"):
        byte = np.frexp(amax)[1] - 1 + 127 - (7 if fmt == "e4m3" else 14)
    else:
        mant, ex = np.frexp(amax / 6.0)
        byte = np.where(mant > 0.5, ex, ex - 1) + 127
    byte = np.clip(np.where(amax > 0, byte, 1), 1, 254)
    scaled = (w * np.exp2(127.0 - byte)[:, None, :]).reshape(k, n).astype(np.float32)
    by_word = np.ascontiguousarray(scaled.reshape(k // 512, 128, 4, n).transpose(0, 1, 3, 2))
    if fmt in ("e4m3", "e5m2"):
        words = by_word.astype(ml_dtypes.float8_e4m3fn if fmt == "e4m3" else ml_dtypes.float8_e5m2).view(np.uint8)
    else:
        c = by_word.astype(ml_dtypes.float4_e2m1fn).view(np.uint8) & 0xF
        words = (c[..., 0::2] | (c[..., 1::2] << 4)).reshape(k // 512, 128, 2 * n)
    return np.ascontiguousarray(words), np.ascontiguousarray(byte.astype(np.uint8).reshape(k // 512, 16, n))


def unpack_weight(words, scales, fmt):
    g, _, n = scales.shape
    words = np.ascontiguousarray(words).reshape(g, 128, n, -1)
    if fmt in ("e4m3", "e5m2"):
        vals = words.view(ml_dtypes.float8_e4m3fn if fmt == "e4m3" else ml_dtypes.float8_e5m2).astype(np.float64)
    else:
        nib = np.empty((g, 128, n, 4), np.uint8)
        nib[..., 0::2] = words & 0xF
        nib[..., 1::2] = words >> 4
        vals = E2M1[nib]
    vals = vals * np.repeat(np.exp2(scales.astype(np.float64) - 127.0), 8, axis=1)[..., None]
    return vals.transpose(0, 1, 3, 2).reshape(g * 512, n)


def bf(x):
    return np.asarray(x, np.float32).astype(ml_dtypes.bfloat16)


def planes(Y):
    r, m = Y.shape
    b = f64(bf(Y)).reshape(r // 32, 32, m)
    amax = np.abs(b).max(1)
    byte = np.clip(np.where(amax > 0, np.frexp(amax)[1] - 1 + 127 - 7, 1), 1, 254)
    codes = (b * np.exp2(127.0 - byte)[:, None, :]).reshape(r, m).astype(np.float32).astype(ml_dtypes.float8_e4m3fn).view(np.uint8)
    words = codes.reshape(r // 512, 128, 4, m).transpose(0, 1, 3, 2)
    return np.ascontiguousarray(words), np.ascontiguousarray(byte.astype(np.uint8).reshape(r // 512, 16, m))


K, F, T, Z, J, R, C, O, N, E = 512, 512, 1024, 1024, 256, 512, 512, 256, 512, 1024


def setup_inputs():
    n = np.random.standard_normal
    idx = np.random.permutation(T)[:J]
    idx2 = np.random.permutation(Z)[:J]
    idx3 = np.random.permutation(C)[:J]
    idx4 = np.random.permutation(C)[:J]
    idx5 = np.random.permutation(C)[:O]
    idx6 = np.random.permutation(C)[:O]
    idx7 = np.random.permutation(E)[:O]
    fk = mx_kscale(K)
    fr = mx_kscale(R)
    ff = mx_kscale(F)
    xtp = pack_weight(n((K, T)) / fk[:, None], "e4m3")
    wp = pack_weight(n((K, R)) * 1 / np.sqrt(K) * fk[:, None] * fr, "e2m1")
    xop = pack_weight(n((F, Z)) / ff[:, None], "e2m1")
    w2p = pack_weight(n((F, R)) * 1 / np.sqrt(F) * ff[:, None] * fr, "e5m2")
    wbp = pack_weight(n((R, N)) * 1 / np.sqrt(R) / fr[:, None], "e5m2")
    return {
        "xt_words": xtp[0],
        "xt_scales": xtp[1],
        "w_words": wp[0],
        "w_scales": wp[1],
        "xo_words": xop[0],
        "xo_scales": xop[1],
        "w2_words": w2p[0],
        "w2_scales": w2p[1],
        "wb_words": wbp[0],
        "wb_scales": wbp[1],
        "tz": (n((N, E))).astype(np.float32),
        "offs": striped(idx),
        "offs2": striped(idx2),
        "offs3": striped(idx3),
        "offs4": striped(idx4),
        "offs5": striped(idx5),
        "offs6": striped(idx6),
        "offs7": striped(idx7),
    }


def reference(xt_words, xt_scales, w_words, w_scales, xo_words, xo_scales, w2_words, w2_scales, wb_words, wb_scales, tz, offs, offs2, offs3, offs4, offs5, offs6, offs7):
    idx = unstriped(offs)
    idx2 = unstriped(offs2)
    idx3 = unstriped(offs3)
    idx4 = unstriped(offs4)
    idx5 = unstriped(offs5)
    idx6 = unstriped(offs6)
    idx7 = unstriped(offs7)
    xtu = unpack_weight(xt_words, xt_scales, "e4m3")
    wu = unpack_weight(w_words, w_scales, "e2m1")
    xou = unpack_weight(xo_words, xo_scales, "e2m1")
    w2u = unpack_weight(w2_words, w2_scales, "e5m2")
    wbu = unpack_weight(wb_words, wb_scales, "e5m2")
    xtidxg = xtu[:, idx]
    a = wu.T @ xtidxg
    xoidx2g = xou[:, idx2]
    b = w2u.T @ xoidx2g
    pw = np.zeros((R, C))
    pw[:, idx3] = a
    pv = np.zeros((R, C))
    pv[:, idx4] = b
    hid = np.maximum(pw[:, idx5], pv[:, idx6])
    hidq = mxq(hid, 0, "e4m3")
    p = wbu.T @ hidq
    y = p + f64(tz)[:, idx7]
    words, scales = planes(y)
    return y, words, scales

from contextlib import ExitStack

import concourse.mybir as mybir

F32 = mybir.dt.float32
BF16 = mybir.dt.bfloat16
I32 = mybir.dt.int32
U32 = mybir.dt.uint32
U16 = mybir.dt.uint16
U8 = mybir.dt.uint8
E4M3 = mybir.dt.float8_e4m3fn_x4
E5M2 = mybir.dt.float8_e5m2_x4
E2M1 = mybir.dt.float4_e2m1fn_x4
COPY = mybir.ActivationFunctionType.Copy
ADD = mybir.AluOpType.add
MAX = mybir.AluOpType.max

P = 128
PACK = 4
TABLE = 1024
SLOTS = 256
FEATURES = 512
BOARD = 512
READS = 256
HALF = READS // 2
RUN = 4

FLOPS = 3 * 2 * 512 * FEATURES * SLOTS


def words32(ap):
    return ap[0].rearrange("p n t -> p (n t)").bitcast(I32)


def tile_list_twotab_twoboards_one_tabled_pl_kernel(
    tc, xt_words, xt_scales, w_words, w_scales, xo_words, xo_scales, w2_words, w2_scales,
    wb_words, wb_scales, tz, offs, offs2, offs3, offs4, offs5, offs6, offs7, out_0, out_1, out_2,
):
    nc = tc.nc
    with ExitStack() as ctx:
        lists = ctx.enter_context(tc.tile_pool(name="lists", bufs=1))
        sb = ctx.enter_context(tc.tile_pool(name="sb", bufs=1))
        ps = ctx.enter_context(tc.psum_pool(name="ps", bufs=1))

        def new(name, shape, dtype, tag=None):
            return sb.tile(shape, dtype, name=name, tag=tag or name, align_bytes=64)

        def load_list(name, src):
            t = lists.tile([P, SLOTS // 16], U16, name=name)
            nc.sync.dma_start(t[:], src)
            return t

        def load_scales(name, src):
            width = src.shape[2]
            t = new(name, [P, width], U8)
            rows = src[0].bitcast(I32)
            for q in range(4):
                nc.sync.dma_start(
                    t[32 * q : 32 * q + 32, :].bitcast(I32), rows[4 * q : 4 * q + 4, :].partition_broadcast(8)
                )
            return t

        def deal(copy, name, src, dtype, tag=None):
            t = new(name, [P, FEATURES], dtype, tag)
            copy(t[:].rearrange("p (t m) -> p m t", t=PACK), src.rearrange("p (m t) -> p m t", t=PACK))
            return t

        def gather(name, window, offsets, dtype):
            t = new(name, [P, SLOTS], dtype)
            nc.vector.tensor_copy(t[:], window.indirect(offsets[:]))
            return t

        def scalar_copy(out, in_):
            nc.scalar.activation(out, in_, COPY)

        xo_w = new("xo_w", [P, TABLE], U16)
        w2_w = new("w2_w", [P, FEATURES], U32)
        xt_w = new("xt_w", [P, TABLE], U32)
        w_w = new("w_w", [P, FEATURES], U16)
        wb_w = new("wb_w", [P, FEATURES], U32)
        tz_t = [new("tz%d" % t, [P, TABLE], F32) for t in range(PACK)]

        xo_s = load_scales("xo_s", xo_scales)
        l2 = load_list("l2", offs2)
        nc.sync.dma_start(xo_w[:].bitcast(I32), xo_words[0].bitcast(I32))
        nc.sync.dma_start(w2_w[:].bitcast(I32), words32(w2_words))
        nc.sync.dma_start(w_w[:].bitcast(I32), w_words[0].bitcast(I32))
        w2_s = load_scales("w2_s", w2_scales)
        l4 = load_list("l4", offs4)
        l1 = load_list("l1", offs)
        nc.sync.dma_start(xt_w[:].bitcast(I32), words32(xt_words))
        xt_s = load_scales("xt_s", xt_scales)
        w_s = load_scales("w_s", w_scales)
        l3 = load_list("l3", offs3)
        nc.sync.dma_start(wb_w[:].bitcast(I32), words32(wb_words))
        wb_s = load_scales("wb_s", wb_scales)
        l6 = load_list("l6", offs6)
        l5 = load_list("l5", offs5)
        l7 = load_list("l7", offs7)
        tz_rows = tz.rearrange("(p t) e -> t p e", t=PACK)
        for t in range(PACK):
            nc.sync.dma_start(tz_t[t][:], tz_rows[t])

        def boards(name):
            tiles = [new("%s%d" % (name, t), [P, BOARD], F32) for t in range(PACK)]
            for b in tiles:
                nc.vector.memset(b[:], 0.0)
            return tiles

        pv = boards("pv")
        pw = boards("pw")

        def first_stage(name, w_words_d, w_fmt, w_scales_d, x_words_g, x_fmt, x_scales_g):
            banks = [ps.tile([P, 2 * SLOTS], F32, name="%s_bank%d" % (name, i)) for i in range(2)]
            for t in range(PACK):
                cols = slice(t * P, (t + 1) * P)
                nc.tensor.matmul_mx(
                    banks[t // 2][:, (t % 2) * SLOTS : (t % 2 + 1) * SLOTS],
                    lhsT=w_words_d[:, cols].bitcast(w_fmt), lhsT_scale=w_scales_d[:, cols],
                    rhs=x_words_g[:].bitcast(x_fmt), rhs_scale=x_scales_g[:],
                    start=True, stop=True,
                )
            return banks

        def put_on_board(name, banks, board, put, plain_copy, listed_copy):
            for i in range(2):
                sums = new("%s_sums%d" % (name, i), [P, 2 * SLOTS], F32)
                plain_copy(sums[:], banks[i][:])
                for u in range(2):
                    t = 2 * i + u
                    listed_copy(board[t][:].indirect(put[:]), sums[:, u * SLOTS : (u + 1) * SLOTS])

        def pick(name, board, offsets, copies, tag=None):
            picked = new(name, [P, PACK, READS], F32, tag)
            for t in range(PACK):
                copies[t](picked[:, t, :], board[t][:].indirect(offsets[:]))
            return picked

        xo_wg = gather("xo_wg", xo_w[:], l2, U16)
        xo_sg = gather("xo_sg", xo_s[:], l2, U8)
        w2_wd = deal(nc.scalar.copy, "w2_wd", w2_w[:], U32)
        w_wd = deal(nc.scalar.copy, "w_wd", w_w[:], U16)
        w2_sd = deal(nc.vector.tensor_copy, "w2_sd", w2_s[:], U8)
        b_banks = first_stage("b", w2_wd, E5M2, w2_sd, xo_wg, E2M1, xo_sg)
        xt_wg = gather("xt_wg", xt_w[:], l1, U32)
        xt_sg = gather("xt_sg", xt_s[:], l1, U8)
        w_sd = deal(nc.vector.tensor_copy, "w_sd", w_s[:], U8)
        a_banks = first_stage("a", w_wd, E2M1, w_sd, xt_wg, E4M3, xt_sg)

        vector_copy = nc.vector.tensor_copy
        put_on_board("b", b_banks, pv, l4, nc.scalar.copy, scalar_copy)
        put_on_board("a", a_banks, pw, l3, vector_copy, vector_copy)
        gv = pick("gv", pv, l6, [scalar_copy] * PACK)
        gw = pick("gw", pw, l5, [scalar_copy, scalar_copy, vector_copy, vector_copy], "b_sums1")

        wb_sd = deal(nc.vector.tensor_copy, "wb_sd", wb_s[:], U8, "a_sums0")
        wb_wd = deal(nc.scalar.copy, "wb_wd", wb_w[:], U32, "b_sums0")

        def by_run(ap):
            return ap.rearrange("p t (c i) -> p c t i", i=RUN)

        def woven(tile_):
            return tile_[:].rearrange("p (c i t) -> p c t i", i=RUN, t=PACK)

        tzg = [new("tzg%d" % h, [P, PACK, HALF], F32, "pw%d" % h) for h in range(2)]
        for h in range(2):
            for t in range(PACK):
                scalar_copy(tzg[h][:, t, :], tz_t[t][:].indirect(l7[:, h * HALF // 16 : (h + 1) * HALF // 16]))

        p_banks = []
        for h in range(2):
            o = slice(h * HALF, (h + 1) * HALF)
            hid = new("hid%d" % h, [P, HALF * PACK], BF16)
            nc.vector.tensor_tensor(woven(hid), by_run(gw[:, :, o]), by_run(gv[:, :, o]), MAX)
            hid_w = new("hid_w%d" % h, [P, HALF], U32)
            hid_s = new("hid_s%d" % h, [P, HALF], U8)
            nc.vector.quantize_mx(hid_w[:].bitcast(E4M3), hid_s[:], hid[:])
            bank = ps.tile([P, PACK, HALF], F32, name="p_bank%d" % h)
            for t in range(PACK):
                cols = slice(t * P, (t + 1) * P)
                nc.tensor.matmul_mx(
                    bank[:, t, :],
                    lhsT=wb_wd[:, cols].bitcast(E5M2), lhsT_scale=wb_sd[:, cols],
                    rhs=hid_w[:].bitcast(E4M3), rhs_scale=hid_s[:],
                    start=True, stop=True,
                )
            p_banks.append(bank)

        y_rows = out_0.rearrange("(p t) o -> p t o", t=PACK)
        y_w = new("y_w", [P, READS], U32)
        y_s = new("y_s", [P, READS], U8)
        out_words = words32(out_1)
        ys = []
        for h in range(2):
            o = slice(h * HALF, (h + 1) * HALF)
            y = new("y%d" % h, [P, PACK, HALF], F32)
            nc.vector.tensor_tensor(y[:], p_banks[h][:], tzg[h][:], ADD)
            nc.sync.dma_start(y_rows[:, :, o], y[:])
            ys.append(y)
        casts = [nc.scalar.copy, nc.vector.tensor_copy]
        for h in range(2):
            o = slice(h * HALF, (h + 1) * HALF)
            yb = new("yb%d" % h, [P, HALF * PACK], BF16)
            casts[h](woven(yb), by_run(ys[h][:]))
            nc.vector.quantize_mx(y_w[:, o].bitcast(E4M3), y_s[:, o], yb[:])
            nc.sync.dma_start(out_words[:, o], y_w[:, o].bitcast(I32))
        scale_rows = out_2[0].bitcast(I32)
        for q in range(4):
            queue = nc.scalar if q % 2 else nc.sync
            queue.dma_start(scale_rows[4 * q : 4 * q + 4, :], y_s[32 * q : 32 * q + 4, :].bitcast(I32))
